import numpy as np
import ml_dtypes


def mxq(x, axis, fmt="e4m3"):
    dtype, down = {"e4m3": (ml_dtypes.float8_e4m3fn, 7), "e5m2": (ml_dtypes.float8_e5m2, 14)}[fmt]
    v = np.moveaxis(np.asarray(x, np.float32).astype(ml_dtypes.bfloat16).astype(np.float64), axis, -1)
    blocks = v.reshape(v.shape[:-1] + (-1, 32))
    amax = np.abs(blocks).max(-1, keepdims=True)
    byte = np.maximum(np.where(amax > 0, np.frexp(amax)[1] - 1 + 127, 0) - down, 1)
    scale = np.exp2(byte - 127.0)
    codes = (blocks / scale).astype(np.float32).astype(dtype).astype(np.float64)
    return np.moveaxis((codes * scale).reshape(v.shape), -1, axis)


WIDE = False


def mx_kscale(k):
    if not WIDE:
        return np.ones(k)
    levels = np.array([10, -10, 5, -5, 0])
    if k % 512:
        return np.exp2(np.random.permutation(np.resize(levels, k // 32))).repeat(32)
    a = np.empty((k // 512, 16))
    for p in range(k // 512):
        a[p, :8] = np.random.permutation(np.resize(levels, 8))
        for g in range(8):
            far = levels[np.abs(levels - a[p, g]) >= 10]
            a[p, g + 8] = far[np.random.randint(len(far))]
    return np.exp2(a.ravel()).repeat(32)


def f64(x):
    return np.asarray(x).astype(np.float64)


def striped(idx):
    return np.tile(idx.reshape(-1, 16).T, (8, 1)).astype(np.uint16)


def unstriped(offs):
    return offs[:16].T.reshape(-1).astype(np.int64)


def striped8(idx):
    return np.concatenate([x.reshape(-1, 16).T for x in idx]).astype(np.uint16)


def runs(offs, k):
    lists = np.stack([offs[16 * r : 16 * r + 16].T.reshape(-1) for r in range(8)]).astype(np.int64)
    return lists[np.arange(k) % 512 // 64]


def pack_weight(w):
    k, n = w.shape
    w = f64(np.asarray(w, np.float32).astype(ml_dtypes.bfloat16)).reshape(k // 32, 32, n)
    amax = np.abs(w).max(1)
    byte = np.clip(np.where(amax > 0, np.frexp(amax)[1] - 1 + 127 - 7, 1), 1, 254)
    scaled = (w * np.exp2(127.0 - byte)[:, None, :]).reshape(k, n).astype(np.float32)
    words = np.ascontiguousarray(scaled.reshape(k // 512, 128, 4, n).transpose(0, 1, 3, 2)).astype(ml_dtypes.float8_e4m3fn).view(np.uint8)
    return words, np.ascontiguousarray(byte.astype(np.uint8).reshape(k // 512, 16, n))


def unpack_weight(words, scales):
    g, p, n, _ = words.shape
    vals = np.ascontiguousarray(words).view(ml_dtypes.float8_e4m3fn).astype(np.float64) * np.repeat(np.exp2(scales.astype(np.float64) - 127.0), 8, axis=1)[..., None]
    return vals.transpose(0, 1, 3, 2).reshape(g * 512, n)


K, T, S, N, H, W, G = 512, 2048, 512, 512, 512, 1024, 2048


def setup_inputs():
    n = np.random.standard_normal
    s = mx_kscale(K)[:, None]
    u = mx_kscale(S)
    packed_xT = pack_weight(n((K, T)) * s)
    packed_dT = pack_weight(n((K, G)) / s)
    return {
        "x_words": packed_xT[0],
        "x_scales": packed_xT[1],
        "w1": (n((K, H)) / np.sqrt(K) / s).astype(np.float32),
        "gn": (np.random.uniform(0.5, 1.5, (H, 1)) * u[:, None]).astype(np.float32),
        "w2": (n((H, N)) / np.sqrt(H) / u[:, None]).astype(np.float32),
        "d_words": packed_dT[0],
        "d_scales": packed_dT[1],
        "offs": striped(np.random.permutation(T)[:S]),
        "n1": striped(np.random.randint(0, S, W)),
        "n2": striped(np.random.permutation(S)),
        "two": striped(np.random.permutation(T)[:S]),
        "k1": striped8(np.random.randint(0, G, (8, H))),
        "n3": striped8(np.stack([np.random.permutation(S) for _ in range(8)])),
        "n4": striped8(np.stack([np.random.permutation(S) for _ in range(8)])),
        "n5": striped8(np.stack([np.random.permutation(S) for _ in range(8)])),
    }


def reference(x_words, x_scales, w1, gn, w2, d_words, d_scales, offs, n1, n2, two, k1, n3, n4, n5):
    d_k1 = unpack_weight(d_words, d_scales)[np.arange(K)[:, None], runs(k1, K)]
    x_two = unpack_weight(x_words, x_scales)[:, unstriped(two)]
    b = 0.0625 * (d_k1.T @ x_two)
    xq = unpack_weight(x_words, x_scales)[:, unstriped(offs)]
    y = mxq(f64(w1), 0, "e4m3").T @ xq
    mb = y[:, unstriped(n1)]
    mx = mb.reshape(H, S, 2).max(axis=2)
    st = y - mx
    z = f64(gn) * (np.maximum(st, st[:, unstriped(n2)]))
    a = mxq(f64(w2), 0, "e4m3").T @ mxq(z, 0, "e4m3")
    return b * (a[np.arange(N)[:, None], runs(n3, N)] - a) + 0.5 * ((b[np.arange(H)[:, None], runs(n5, H)]) * (a[np.arange(N)[:, None], runs(n4, N)] - a))

@@ -1,0 +1,276 @@
+from contextlib import ExitStack
+
+import concourse.mybir as mybir
+
+K, T, S, N, H, W, G = 512, 2048, 512, 512, 512, 1024, 2048
+FLOPS = 3 * 2 * 512 * 512 * 512
+
+F32 = mybir.dt.float32
+BF16 = mybir.dt.bfloat16
+I32 = mybir.dt.int32
+U32 = mybir.dt.uint32
+U16 = mybir.dt.uint16
+U8 = mybir.dt.uint8
+FP8X4 = mybir.dt.float8_e4m3fn_x4
+ALU = mybir.AluOpType
+COPY = mybir.ActivationFunctionType.Copy
+
+P = 128
+PACK = 4
+SPARE = 16
+ORDER = (3, 2, 1, 0)
+VG = (2, 1, 0)
+
+
+def tile_picked_cdjoinflowbghopm_none_p_kernel(
+    tc, x_words, x_scales, w1, gn, w2, d_words, d_scales, offs, n1, n2, two, k1, n3, n4, n5, out
+):
+    nc = tc.nc
+    with ExitStack() as ctx:
+        keep = ctx.enter_context(tc.tile_pool(name="keep", bufs=1))
+        ring = ctx.enter_context(tc.tile_pool(name="ring", bufs=3))
+        psum = ctx.enter_context(tc.psum_pool(name="psum", bufs=1))
+
+        def sb(name, shape, dtype):
+            return keep.tile(shape, dtype, name=name, align_bytes=64)
+
+        def load_list(name, src):
+            tile = keep.tile(list(src.shape), U16, name=name)
+            nc.sync.dma_start(tile[:], src)
+            return tile
+
+        def load_scale_rows(queue, tile, scales, places):
+            rows = scales[0].bitcast(I32).rearrange("(q r) n -> r q n", r=4)
+            for r, place in enumerate(places):
+                queue.dma_start(tile[place:P:32, :].bitcast(I32), rows[r])
+
+        def load_words(tile, words):
+            nc.sync.dma_start(tile[:].bitcast(I32), words[0].rearrange("p n t -> p (n t)").bitcast(I32))
+
+        def gather(on_vector, dst, window, offsets):
+            if on_vector:
+                nc.vector.tensor_copy(dst, window.indirect(offsets))
+            else:
+                nc.scalar.activation(dst, window.indirect(offsets), COPY)
+
+        def mx(bank, codes, scales, t, rhs_codes, rhs_scales):
+            cols = slice(t * P, (t + 1) * P)
+            nc.tensor.matmul_mx(
+                out=bank,
+                lhsT=codes[:, cols].bitcast(FP8X4),
+                lhsT_scale=scales[:, cols],
+                rhs=rhs_codes.bitcast(FP8X4),
+                rhs_scale=rhs_scales,
+                start=True,
+                stop=True,
+            )
+
+        x_scale_table = sb("x_scale_table", [P, T], U8)
+        d_scale_table = sb("d_scale_table", [P, G], U8)
+        x_word_table = sb("x_word_table", [P, T], U32)
+        d_word_table = sb("d_word_table", [P, G], U32)
+        st_all = sb("st_all", [P, (PACK + 1) * S], F32)
+        st2_all = sb("st2_all", [P, PACK * S], F32)
+        b_win = [sb("b_win%d" % t, [P, 2 * S], F32) for t in range(PACK)]
+        a_win = {t: sb("a_win%d" % t, [P, 2 * S], F32) for t in (0, 2, 3)}
+        y_win = [b_win[0]] + [sb("y_win%d" % t, [P, S + SPARE], F32) for t in (1, 2, 3)]
+        larger = {3: b_win[0][:, S:], 2: b_win[3][:, S:], 1: b_win[2][:, S:], }
+        d_scale_placed = sb("d_scale_placed", [P, H], U8)
+
+        nc.gpsimd.memset(x_scale_table[:].bitcast(I32), 0)
+        nc.vector.memset(d_scale_table[:].bitcast(I32), 0)
+        for t in (3, 2, 1):
+            nc.gpsimd.memset(y_win[t][:, S:], 0.0)
+        nc.gpsimd.memset(b_win[1][:, S:], 0.0)
+        nc.gpsimd.memset(st_all[:, PACK * S :], 0.0)
+        nc.gpsimd.memset(d_scale_placed[:].bitcast(I32), 0)
+
+        offs_l = load_list("offs_l", offs)
+        two_l = load_list("two_l", two)
+        load_scale_rows(nc.sync, x_scale_table, x_scales, (0, 1, 2, 3))
+        w1_raw = sb("w1_raw", [P, PACK, H], F32)
+        nc.sync.dma_start(w1_raw[:], w1.rearrange("(p j) c -> p j c", j=PACK))
+        load_words(x_word_table, x_words)
+        gain = sb("gain", [P, PACK], F32)
+        nc.sync.dma_start(gain[:], gn.rearrange("(p t) o -> p (t o)", t=PACK))
+        k1_l = load_list("k1_l", k1)
+        n1_l = load_list("n1_l", n1)
+        load_words(d_word_table, d_words)
+        load_scale_rows(nc.sync, d_scale_table, d_scales, (0, 1, 16, 17))
+        n2_l = load_list("n2_l", n2)
+        w2_raw = sb("w2_raw", [P, PACK, N], F32)
+        nc.sync.dma_start(w2_raw[:], w2.rearrange("(p j) c -> p j c", j=PACK))
+        n5_l = load_list("n5_l", n5)
+        n3_l = load_list("n3_l", n3)
+        n4_l = load_list("n4_l", n4)
+
+        twice_nonneg = sb("twice_nonneg", [P, PACK], F32)
+        gain_sign = sb("gain_sign", [P, PACK], F32)
+        gain_size = sb("gain_size", [P, PACK], F32)
+        nc.gpsimd.tensor_scalar(twice_nonneg[:], gain[:], 0.0, 2.0, ALU.is_ge, ALU.mult)
+        nc.gpsimd.tensor_scalar(gain_sign[:], twice_nonneg[:], 1.0, -1.0, ALU.mult, ALU.add)
+        nc.scalar.activation(gain_size[:], gain[:], mybir.ActivationFunctionType.Abs)
+
+        xo_scales = sb("xo_scales", [P, S], U8)
+        xo_words = sb("xo_words", [P, S], U32)
+        nc.vector.tensor_copy(xo_scales[:], x_scale_table[:].indirect(offs_l[:]))
+        nc.vector.tensor_copy(xo_words[:], x_word_table[:].indirect(offs_l[:]))
+
+        w1_bf = sb("w1_bf", [P, PACK, P, PACK], BF16)
+        halves = w1_bf[:].rearrange("p t (h m) j -> p h m j t", h=2)
+        raw_halves = w1_raw[:].rearrange("p j (h m t) -> p h m j t", h=2, t=PACK)
+        nc.scalar.activation(halves[:, 0], raw_halves[:, 0], COPY)
+        nc.vector.tensor_copy(halves[:, 1], raw_halves[:, 1])
+        w1_codes = sb("w1_codes", [P, H], U32)
+        w1_scales = sb("w1_scales", [P, H], U8)
+        for t in ORDER:
+            cols = slice(t * P, (t + 1) * P)
+            nc.vector.quantize_mx(
+                out=w1_codes[:, cols].bitcast(FP8X4),
+                scales=w1_scales[:, cols],
+                in_=w1_bf[:, t].rearrange("p m j -> p (m j)"),
+            )
+
+        def project(t):
+            y_bank = psum.tile([P, S], F32, name="y_bank", tag="bank%d" % t)
+            mx(y_bank[:], w1_codes, w1_scales, t, xo_words[:], xo_scales[:])
+            nc.scalar.activation(y_win[t][:, :S], y_bank[:], COPY, scale=gain_size[:, t : t + 1])
+
+        xt_scales = sb("xt_scales", [P, S], U8)
+        xt_words = sb("xt_words", [P, S], U32)
+        dk_scales = sb("dk_scales", [P, H], U8)
+        dk_words = sb("dk_words", [P, H], U32)
+        dk_scales_dealt = sb("dk_scales_dealt", [P, H], U8)
+        dk_words_dealt = sb("dk_words_dealt", [P, H], U32)
+        nc.vector.tensor_copy(xt_scales[:], x_scale_table[:].indirect(two_l[:]))
+        nc.vector.tensor_copy(xt_words[:], x_word_table[:].indirect(two_l[:]))
+
+        def pick_code_scales():
+            nc.vector.tensor_copy(dk_scales[:], d_scale_table[:].indirect(k1_l[:]))
+            nc.vector.tensor_copy(
+                dk_scales_dealt[:].rearrange("p (t m) -> p m t", t=PACK),
+                dk_scales[:].rearrange("p (m t) -> p m t", t=PACK),
+            )
+            for r, place in enumerate((0, 1, 16, 17)):
+                nc.sync.dma_start(d_scale_placed[r:P:32, :].bitcast(I32), dk_scales_dealt[place:P:32, :].bitcast(I32))
+
+        def pick_code_words():
+            nc.vector.tensor_copy(dk_words[:], d_word_table[:].indirect(k1_l[:]))
+            nc.vector.tensor_copy(
+                dk_words_dealt[:].rearrange("p (t m) -> p m t", t=PACK),
+                dk_words[:].rearrange("p (m t) -> p m t", t=PACK),
+            )
+
+        def members(t):
+            mb = ring.tile([P, W], F32, name="mb")
+            for h in range(2):
+                gather(h == 1 and t in VG, mb[:, h * S : (h + 1) * S], y_win[t][:], n1_l[:, h * 32 : (h + 1) * 32])
+            return mb
+
+        def difference_last(mb):
+            pairs = mb[:].rearrange("p (h j e) -> p h e j", h=2, e=2)
+            held = [a_win[3][:, S : S + S // 2], a_win[2][:, S : S + S // 2]]
+            for h in range(2):
+                nc.vector.tensor_tensor(held[h], pairs[:, h, 0], pairs[:, h, 1], ALU.max)
+            for h in range(2):
+                cols = slice(h * (S // 2), (h + 1) * (S // 2))
+                nc.vector.tensor_tensor(st_all[:, cols], y_win[0][:, cols], held[h], ALU.subtract)
+
+        def difference(t, mb):
+            pairs = mb[:].rearrange("p (j e) -> p e j", e=2)
+            nc.vector.tensor_tensor(larger[t], pairs[:, 0], pairs[:, 1], ALU.max)
+            nc.vector.tensor_tensor(st_all[:, t * S : (t + 1) * S], y_win[t][:, :S], larger[t], ALU.subtract)
+
+        def partner(t):
+            gather(False, st2_all[:, t * S : (t + 1) * S], st_all[:, t * S : (t + 2) * S], n2_l[:])
+
+        w2_bf = sb("w2_bf", [P, PACK, P, PACK], BF16)
+        w2_codes = sb("w2_codes", [P, N], U32)
+        w2_scales = sb("w2_scales", [P, N], U8)
+
+        def quantize_w2():
+            nc.vector.tensor_tensor(
+                w2_bf[:].rearrange("p t m j -> p m j t"),
+                w2_raw[:].rearrange("p j (m t) -> p m j t", t=PACK),
+                gain_sign[:].unsqueeze(1).unsqueeze(3).to_broadcast([P, P, PACK, PACK]),
+                ALU.mult,
+            )
+            nc.vector.quantize_mx(
+                out=w2_codes[:].bitcast(FP8X4), scales=w2_scales[:], in_=w2_bf[:].rearrange("p t m j -> p (t m j)")
+            )
+
+        def coded(t):
+            b_bank = psum.tile([P, S], F32, name="b_bank", tag="bank%d" % (PACK + t))
+            mx(b_bank[:], dk_words_dealt, d_scale_placed, t, xt_words[:], xt_scales[:])
+            nc.scalar.activation(b_win[t][:, :S], b_bank[:], COPY, scale=0.0625)
+
+        def fetch_coded(t):
+            gather(t == 1, a_win[t][:, S:], b_win[t][:], n5_l[:])
+
+        mbs = {}
+        project(3)
+        mbs[3] = members(3)
+        project(2)
+        pick_code_words()
+        mbs[2] = members(2)
+        pick_code_scales()
+        difference(3, mbs[3])
+        partner(3)
+        project(1)
+        mbs[1] = members(1)
+        difference(2, mbs[2])
+        partner(2)
+        project(0)
+        mbs[0] = members(0)
+        difference(1, mbs[1])
+        partner(1)
+        difference_last(mbs[0])
+        partner(0)
+        quantize_w2()
+        coded(3)
+        coded(2)
+        coded(1)
+        fetch_coded(3)
+        fetch_coded(2)
+
+        z_codes = sb("z_codes", [P, S], U32)
+        z_scales = sb("z_scales", [P, S], U8)
+        z_bf = [keep.tile([P, S // 2, PACK], BF16, name="z_bf", tag="z_bf%d" % h, align_bytes=64) for h in range(2)]
+        st_view = st_all[:, : PACK * S].rearrange("p (t h c i) -> p h c t i", t=PACK, h=2, i=4)
+        st2_view = st2_all[:].rearrange("p (t h c i) -> p h c t i", t=PACK, h=2, i=4)
+        for h in range(2):
+            z_view = z_bf[h][:].rearrange("p (c i) t -> p c t i", i=4)
+            nc.vector.tensor_tensor(z_view, st_view[:, h], st2_view[:, h], ALU.max)
+        for h in range(2):
+            cols = slice(h * (S // 2), (h + 1) * (S // 2))
+            nc.vector.quantize_mx(
+                out=z_codes[:, cols].bitcast(FP8X4),
+                scales=z_scales[:, cols],
+                in_=z_bf[h][:].rearrange("p c t -> p (c t)"),
+            )
+        a_win[1] = keep.tile([P, 2 * S], F32, name="a_win1", tag="z_bf1", align_bytes=64)
+        fetch_coded(1)
+
+        out_rows = out.rearrange("(p t) n -> t p n", t=PACK)
+        for t in ORDER:
+            a_bank = psum.tile([P, S], F32, name="a_bank", tag="bank%d" % t)
+            mx(a_bank[:], w2_codes, w2_scales, t, z_codes[:], z_scales[:])
+            nc.scalar.activation(a_win[t][:, :S], a_bank[:], COPY)
+            if t == 2:
+                coded(0)
+                fetch_coded(0)
+            at_n3 = ring.tile([P, S], F32, name="at_n3")
+            at_n4 = ring.tile([P, S], F32, name="at_n4")
+            gather(False, at_n3[:], a_win[t][:], n3_l[:])
+            gather(t == 3, at_n4[:], a_win[t][:], n4_l[:])
+            step3 = ring.tile([P, S], F32, name="step3")
+            step4 = ring.tile([P, S], F32, name="step4")
+            nc.vector.tensor_tensor(step3[:], at_n3[:], a_win[t][:, :S], ALU.subtract)
+            nc.vector.tensor_tensor(step4[:], at_n4[:], a_win[t][:, :S], ALU.subtract)
+            first = ring.tile([P, S], F32, name="first")
+            second = ring.tile([P, S], F32, name="second")
+            result = ring.tile([P, S], F32, name="result")
+            nc.vector.tensor_tensor(first[:], step3[:], b_win[t][:, :S], ALU.mult)
+            nc.vector.tensor_tensor(second[:], step4[:], a_win[t][:, S:], ALU.mult)
+            nc.vector.scalar_tensor_tensor(result[:], second[:], 0.5, first[:], ALU.mult, ALU.add)
+            nc.sync.dma_start(out_rows[t], result[:])

@@ -20,6 +20,7 @@ PACK = 4
 SPARE = 16
 ORDER = (3, 2, 1, 0)
 VG = (2, 1, 0)
+VG4 = (3, 2)
 
 
 def tile_picked_cdjoinflowbghopm_none_p_kernel(
@@ -117,10 +118,9 @@ def tile_picked_cdjoinflowbghopm_none_p_kernel(
         nc.vector.tensor_copy(xo_words[:], x_word_table[:].indirect(offs_l[:]))
 
         w1_bf = sb("w1_bf", [P, PACK, P, PACK], BF16)
-        halves = w1_bf[:].rearrange("p t (h m) j -> p h m j t", h=2)
-        raw_halves = w1_raw[:].rearrange("p j (h m t) -> p h m j t", h=2, t=PACK)
-        nc.scalar.activation(halves[:, 0], raw_halves[:, 0], COPY)
-        nc.vector.tensor_copy(halves[:, 1], raw_halves[:, 1])
+        nc.vector.tensor_copy(
+            w1_bf[:].rearrange("p t m j -> p m j t"), w1_raw[:].rearrange("p j (m t) -> p m j t", t=PACK)
+        )
         w1_codes = sb("w1_codes", [P, H], U32)
         w1_scales = sb("w1_scales", [P, H], U8)
         for t in ORDER:
@@ -199,10 +199,13 @@ def tile_picked_cdjoinflowbghopm_none_p_kernel(
                 out=w2_codes[:].bitcast(FP8X4), scales=w2_scales[:], in_=w2_bf[:].rearrange("p t m j -> p (t m j)")
             )
 
+        b_banks = {}
+
         def coded(t):
             b_bank = psum.tile([P, S], F32, name="b_bank", tag="bank%d" % (PACK + t))
             mx(b_bank[:], dk_words_dealt, d_scale_placed, t, xt_words[:], xt_scales[:])
-            nc.scalar.activation(b_win[t][:, :S], b_bank[:], COPY, scale=0.0625)
+            nc.scalar.activation(b_win[t][:, :S], b_bank[:], COPY, scale=0.5 * 0.0625)
+            b_banks[t] = b_bank
 
         def fetch_coded(t):
             gather(t == 1, a_win[t][:, S:], b_win[t][:], n5_l[:])
@@ -261,16 +264,17 @@ def tile_picked_cdjoinflowbghopm_none_p_kernel(
                 fetch_coded(0)
             at_n3 = ring.tile([P, S], F32, name="at_n3")
             at_n4 = ring.tile([P, S], F32, name="at_n4")
-            gather(False, at_n3[:], a_win[t][:], n3_l[:])
-            gather(t == 3, at_n4[:], a_win[t][:], n4_l[:])
             step3 = ring.tile([P, S], F32, name="step3")
             step4 = ring.tile([P, S], F32, name="step4")
-            nc.vector.tensor_tensor(step3[:], at_n3[:], a_win[t][:, :S], ALU.subtract)
-            nc.vector.tensor_tensor(step4[:], at_n4[:], a_win[t][:, :S], ALU.subtract)
             first = ring.tile([P, S], F32, name="first")
             second = ring.tile([P, S], F32, name="second")
             result = ring.tile([P, S], F32, name="result")
-            nc.vector.tensor_tensor(first[:], step3[:], b_win[t][:, :S], ALU.mult)
-            nc.vector.tensor_tensor(second[:], step4[:], a_win[t][:, S:], ALU.mult)
-            nc.vector.scalar_tensor_tensor(result[:], second[:], 0.5, first[:], ALU.mult, ALU.add)
+            closer = nc.vector if t == 0 else nc.gpsimd
+            gather(t in VG4, at_n4[:], a_win[t][:], n4_l[:])
+            gather(False, at_n3[:], a_win[t][:], n3_l[:])
+            nc.vector.tensor_tensor(step4[:], at_n4[:], a_bank[:], ALU.subtract)
+            closer.tensor_tensor(second[:], step4[:], a_win[t][:, S:], ALU.mult)
+            nc.vector.tensor_tensor(step3[:], at_n3[:], a_bank[:], ALU.subtract)
+            nc.vector.scalar_tensor_tensor(first[:], b_banks[t][:], 0.0625, step3[:], ALU.mult, ALU.mult)
+            closer.tensor_tensor(result[:], first[:], second[:], ALU.add)
             nc.sync.dma_start(out_rows[t], result[:])

@@ -19,8 +19,16 @@ P = 128
 PACK = 4
 SPARE = 16
 ORDER = (3, 2, 1, 0)
-VG = (2, 1, 0)
-VG4 = (3, 2)
+WQ = 1
+VEV = (3,)
+SM = 48
+VR = (1, 0)
+VG3 = (3,)
+LASTP = 1
+GS4 = ()
+VG5 = (1,)
+VG = (3, 1, 0)
+VG4 = (3,)
 
 
 def tile_picked_cdjoinflowbghopm_none_p_kernel(
@@ -29,7 +37,7 @@ def tile_picked_cdjoinflowbghopm_none_p_kernel(
     nc = tc.nc
     with ExitStack() as ctx:
         keep = ctx.enter_context(tc.tile_pool(name="keep", bufs=1))
-        ring = ctx.enter_context(tc.tile_pool(name="ring", bufs=3))
+        ring = ctx.enter_context(tc.tile_pool(name="ring", bufs=4))
         psum = ctx.enter_context(tc.psum_pool(name="psum", bufs=1))
 
         def sb(name, shape, dtype):
@@ -80,8 +88,9 @@ def tile_picked_cdjoinflowbghopm_none_p_kernel(
 
         nc.gpsimd.memset(x_scale_table[:].bitcast(I32), 0)
         nc.vector.memset(d_scale_table[:].bitcast(I32), 0)
-        for t in (3, 2, 1):
+        for t in (2, 1):
             nc.gpsimd.memset(y_win[t][:, S:], 0.0)
+        nc.scalar.activation(y_win[3][:, S:], y_win[2][:, S:], COPY)
         nc.gpsimd.memset(b_win[1][:, S:], 0.0)
         nc.gpsimd.memset(st_all[:, PACK * S :], 0.0)
         nc.gpsimd.memset(d_scale_placed[:].bitcast(I32), 0)
@@ -95,9 +104,9 @@ def tile_picked_cdjoinflowbghopm_none_p_kernel(
         gain = sb("gain", [P, PACK], F32)
         nc.sync.dma_start(gain[:], gn.rearrange("(p t) o -> p (t o)", t=PACK))
         k1_l = load_list("k1_l", k1)
-        n1_l = load_list("n1_l", n1)
+        nc.sync.dma_start(d_scale_table[0:P:8, :].bitcast(I32), d_scales[0].bitcast(I32))
         load_words(d_word_table, d_words)
-        load_scale_rows(nc.sync, d_scale_table, d_scales, (0, 1, 16, 17))
+        n1_l = load_list("n1_l", n1)
         n2_l = load_list("n2_l", n2)
         w2_raw = sb("w2_raw", [P, PACK, N], F32)
         nc.sync.dma_start(w2_raw[:], w2.rearrange("(p j) c -> p j c", j=PACK))
@@ -118,9 +127,10 @@ def tile_picked_cdjoinflowbghopm_none_p_kernel(
         nc.vector.tensor_copy(xo_words[:], x_word_table[:].indirect(offs_l[:]))
 
         w1_bf = sb("w1_bf", [P, PACK, P, PACK], BF16)
-        nc.vector.tensor_copy(
-            w1_bf[:].rearrange("p t m j -> p m j t"), w1_raw[:].rearrange("p j (m t) -> p m j t", t=PACK)
-        )
+        w1_dealt = w1_bf[:].rearrange("p t m j -> p m j t")
+        w1_rows = w1_raw[:].rearrange("p j (m t) -> p m j t", t=PACK)
+        nc.scalar.activation(w1_dealt[:, :SM], w1_rows[:, :SM], COPY)
+        nc.vector.tensor_copy(w1_dealt[:, SM:], w1_rows[:, SM:])
         w1_codes = sb("w1_codes", [P, H], U32)
         w1_scales = sb("w1_scales", [P, H], U8)
         for t in ORDER:
@@ -147,15 +157,19 @@ def tile_picked_cdjoinflowbghopm_none_p_kernel(
 
         def pick_code_scales():
             nc.vector.tensor_copy(dk_scales[:], d_scale_table[:].indirect(k1_l[:]))
+
+        def deal_code_scales():
             nc.vector.tensor_copy(
                 dk_scales_dealt[:].rearrange("p (t m) -> p m t", t=PACK),
                 dk_scales[:].rearrange("p (m t) -> p m t", t=PACK),
             )
-            for r, place in enumerate((0, 1, 16, 17)):
+            for r, place in enumerate((0, 8, 16, 24)):
                 nc.sync.dma_start(d_scale_placed[r:P:32, :].bitcast(I32), dk_scales_dealt[place:P:32, :].bitcast(I32))
 
         def pick_code_words():
             nc.vector.tensor_copy(dk_words[:], d_word_table[:].indirect(k1_l[:]))
+
+        def deal_code_words():
             nc.vector.tensor_copy(
                 dk_words_dealt[:].rearrange("p (t m) -> p m t", t=PACK),
                 dk_words[:].rearrange("p (m t) -> p m t", t=PACK),
@@ -169,7 +183,8 @@ def tile_picked_cdjoinflowbghopm_none_p_kernel(
 
         def difference_last(mb):
             pairs = mb[:].rearrange("p (h j e) -> p h e j", h=2, e=2)
-            held = [a_win[3][:, S : S + S // 2], a_win[2][:, S : S + S // 2]]
+            late_half = keep.tile([P, S // 2], F32, name="late_half", tag="w2_bf", align_bytes=64)
+            held = [b_win[3][:, : S // 2], late_half[:]]
             for h in range(2):
                 nc.vector.tensor_tensor(held[h], pairs[:, h, 0], pairs[:, h, 1], ALU.max)
             for h in range(2):
@@ -184,19 +199,22 @@ def tile_picked_cdjoinflowbghopm_none_p_kernel(
         def partner(t):
             gather(False, st2_all[:, t * S : (t + 1) * S], st_all[:, t * S : (t + 2) * S], n2_l[:])
 
-        w2_bf = sb("w2_bf", [P, PACK, P, PACK], BF16)
+        late = {}
         w2_codes = sb("w2_codes", [P, N], U32)
         w2_scales = sb("w2_scales", [P, N], U8)
 
+        def round_w2():
+            w2_bf = keep.tile([P, PACK, P, PACK], BF16, name="w2_bf", tag="w2_bf", align_bytes=64)
+            late["w2_bf"] = w2_bf
+            dealt = w2_bf[:].rearrange("p t (q m) j -> p q m j t", q=WQ)
+            raw = w2_raw[:].rearrange("p j (q m t) -> p q m j t", q=WQ, t=PACK)
+            sign = gain_sign[:].unsqueeze(1).unsqueeze(3).to_broadcast([P, P // WQ, PACK, PACK])
+            for q in range(WQ):
+                nc.vector.tensor_tensor(dealt[:, q], raw[:, q], sign, ALU.mult)
+
         def quantize_w2():
-            nc.vector.tensor_tensor(
-                w2_bf[:].rearrange("p t m j -> p m j t"),
-                w2_raw[:].rearrange("p j (m t) -> p m j t", t=PACK),
-                gain_sign[:].unsqueeze(1).unsqueeze(3).to_broadcast([P, P, PACK, PACK]),
-                ALU.mult,
-            )
             nc.vector.quantize_mx(
-                out=w2_codes[:].bitcast(FP8X4), scales=w2_scales[:], in_=w2_bf[:].rearrange("p t m j -> p (t m j)")
+                out=w2_codes[:].bitcast(FP8X4), scales=w2_scales[:], in_=late["w2_bf"][:].rearrange("p t m j -> p (t m j)")
             )
 
         b_banks = {}
@@ -208,15 +226,13 @@ def tile_picked_cdjoinflowbghopm_none_p_kernel(
             b_banks[t] = b_bank
 
         def fetch_coded(t):
-            gather(t == 1, a_win[t][:, S:], b_win[t][:], n5_l[:])
+            gather(t in VG5, a_win[t][:, S:], b_win[t][:], n5_l[:])
 
         mbs = {}
         project(3)
         mbs[3] = members(3)
         project(2)
-        pick_code_words()
         mbs[2] = members(2)
-        pick_code_scales()
         difference(3, mbs[3])
         partner(3)
         project(1)
@@ -229,6 +245,11 @@ def tile_picked_cdjoinflowbghopm_none_p_kernel(
         partner(1)
         difference_last(mbs[0])
         partner(0)
+        pick_code_scales()
+        pick_code_words()
+        deal_code_scales()
+        deal_code_words()
+        round_w2()
         quantize_w2()
         coded(3)
         coded(2)
@@ -255,26 +276,51 @@ def tile_picked_cdjoinflowbghopm_none_p_kernel(
         fetch_coded(1)
 
         out_rows = out.rearrange("(p t) n -> t p n", t=PACK)
-        for t in ORDER:
+        a_banks, seconds = {}, {}
+
+        def second_term(t):
             a_bank = psum.tile([P, S], F32, name="a_bank", tag="bank%d" % t)
             mx(a_bank[:], w2_codes, w2_scales, t, z_codes[:], z_scales[:])
-            nc.scalar.activation(a_win[t][:, :S], a_bank[:], COPY)
+            if t in VEV:
+                nc.vector.tensor_copy(a_win[t][:, :S], a_bank[:])
+            else:
+                nc.scalar.activation(a_win[t][:, :S], a_bank[:], COPY)
             if t == 2:
                 coded(0)
                 fetch_coded(0)
-            at_n3 = ring.tile([P, S], F32, name="at_n3")
             at_n4 = ring.tile([P, S], F32, name="at_n4")
-            step3 = ring.tile([P, S], F32, name="step3")
             step4 = ring.tile([P, S], F32, name="step4")
-            first = ring.tile([P, S], F32, name="first")
             second = ring.tile([P, S], F32, name="second")
-            result = ring.tile([P, S], F32, name="result")
-            closer = nc.vector if t == 0 else nc.gpsimd
             gather(t in VG4, at_n4[:], a_win[t][:], n4_l[:])
-            gather(False, at_n3[:], a_win[t][:], n3_l[:])
             nc.vector.tensor_tensor(step4[:], at_n4[:], a_bank[:], ALU.subtract)
-            closer.tensor_tensor(second[:], step4[:], a_win[t][:, S:], ALU.mult)
-            nc.vector.tensor_tensor(step3[:], at_n3[:], a_bank[:], ALU.subtract)
-            nc.vector.scalar_tensor_tensor(first[:], b_banks[t][:], 0.0625, step3[:], ALU.mult, ALU.mult)
-            closer.tensor_tensor(result[:], first[:], second[:], ALU.add)
-            nc.sync.dma_start(out_rows[t], result[:])
+            nc.gpsimd.tensor_tensor(second[:], step4[:], a_win[t][:, S:], ALU.mult)
+            a_banks[t], seconds[t] = a_bank, second
+
+        def first_term(t):
+            at_n3 = ring.tile([P, S], F32, name="at_n3")
+            step3 = ring.tile([P, S], F32, name="step3")
+            first = ring.tile([P, S], F32, name="first")
+            result = ring.tile([P, S], F32, name="result")
+            closer = nc.vector if t in VR else nc.gpsimd
+            pieces = LASTP if t == 0 else 1
+            width = S // pieces
+            spans = [slice(k * width, (k + 1) * width) for k in range(pieces)]
+            for cols in spans:
+                gather(t in VG3, at_n3[:, cols], a_win[t][:], n3_l[:, cols.start // 16 : cols.stop // 16])
+                nc.vector.tensor_tensor(step3[:, cols], at_n3[:, cols], a_banks[t][:, cols], ALU.subtract)
+            for cols in spans:
+                nc.vector.scalar_tensor_tensor(
+                    first[:, cols], b_banks[t][:, cols], 0.0625, step3[:, cols], ALU.mult, ALU.mult
+                )
+            for cols in spans:
+                closer.tensor_tensor(result[:, cols], first[:, cols], seconds[t][:, cols], ALU.add)
+                nc.sync.dma_start(out_rows[t][:, cols], result[:, cols])
+
+        second_term(3)
+        first_term(3)
+        second_term(2)
+        first_term(2)
+        second_term(1)
+        first_term(1)
+        second_term(0)
+        first_term(0)

from contextlib import ExitStack

import concourse.mybir as mybir

K, T, S, N, H, W, G = 512, 2048, 512, 512, 512, 1024, 2048
FLOPS = 3 * 2 * 512 * 512 * 512

F32 = mybir.dt.float32
BF16 = mybir.dt.bfloat16
I32 = mybir.dt.int32
U32 = mybir.dt.uint32
U16 = mybir.dt.uint16
U8 = mybir.dt.uint8
FP8X4 = mybir.dt.float8_e4m3fn_x4
ALU = mybir.AluOpType
COPY = mybir.ActivationFunctionType.Copy

P = 128
PACK = 4
SPARE = 16
ORDER = (3, 2, 1, 0)
WQ = 1
VEV = (3,)
SM = 48
VR = (1, 0)
VG3 = (3,)
LASTP = 1
GS4 = ()
VG5 = (1,)
VG = (3, 1, 0)
VG4 = (3,)


def tile_picked_cdjoinflowbghopm_none_p_kernel(
    tc, x_words, x_scales, w1, gn, w2, d_words, d_scales, offs, n1, n2, two, k1, n3, n4, n5, out
):
    nc = tc.nc
    with ExitStack() as ctx:
        keep = ctx.enter_context(tc.tile_pool(name="keep", bufs=1))
        ring = ctx.enter_context(tc.tile_pool(name="ring", bufs=4))
        psum = ctx.enter_context(tc.psum_pool(name="psum", bufs=1))

        def sb(name, shape, dtype):
            return keep.tile(shape, dtype, name=name, align_bytes=64)

        def load_list(name, src):
            tile = keep.tile(list(src.shape), U16, name=name)
            nc.sync.dma_start(tile[:], src)
            return tile

        def load_scale_rows(queue, tile, scales, places):
            rows = scales[0].bitcast(I32).rearrange("(q r) n -> r q n", r=4)
            for r, place in enumerate(places):
                queue.dma_start(tile[place:P:32, :].bitcast(I32), rows[r])

        def load_words(tile, words):
            nc.sync.dma_start(tile[:].bitcast(I32), words[0].rearrange("p n t -> p (n t)").bitcast(I32))

        def gather(on_vector, dst, window, offsets):
            if on_vector:
                nc.vector.tensor_copy(dst, window.indirect(offsets))
            else:
                nc.scalar.activation(dst, window.indirect(offsets), COPY)

        def mx(bank, codes, scales, t, rhs_codes, rhs_scales):
            cols = slice(t * P, (t + 1) * P)
            nc.tensor.matmul_mx(
                out=bank,
                lhsT=codes[:, cols].bitcast(FP8X4),
                lhsT_scale=scales[:, cols],
                rhs=rhs_codes.bitcast(FP8X4),
                rhs_scale=rhs_scales,
                start=True,
                stop=True,
            )

        x_scale_table = sb("x_scale_table", [P, T], U8)
        d_scale_table = sb("d_scale_table", [P, G], U8)
        x_word_table = sb("x_word_table", [P, T], U32)
        d_word_table = sb("d_word_table", [P, G], U32)
        st_all = sb("st_all", [P, (PACK + 1) * S], F32)
        st2_all = sb("st2_all", [P, PACK * S], F32)
        b_win = [sb("b_win%d" % t, [P, 2 * S], F32) for t in range(PACK)]
        a_win = {t: sb("a_win%d" % t, [P, 2 * S], F32) for t in (0, 2, 3)}
        y_win = [b_win[0]] + [sb("y_win%d" % t, [P, S + SPARE], F32) for t in (1, 2, 3)]
        larger = {3: b_win[0][:, S:], 2: b_win[3][:, S:], 1: b_win[2][:, S:], }
        d_scale_placed = sb("d_scale_placed", [P, H], U8)

        nc.gpsimd.memset(x_scale_table[:].bitcast(I32), 0)
        nc.vector.memset(d_scale_table[:].bitcast(I32), 0)
        for t in (2, 1):
            nc.gpsimd.memset(y_win[t][:, S:], 0.0)
        nc.scalar.activation(y_win[3][:, S:], y_win[2][:, S:], COPY)
        nc.gpsimd.memset(b_win[1][:, S:], 0.0)
        nc.gpsimd.memset(st_all[:, PACK * S :], 0.0)
        nc.gpsimd.memset(d_scale_placed[:].bitcast(I32), 0)

        offs_l = load_list("offs_l", offs)
        two_l = load_list("two_l", two)
        load_scale_rows(nc.sync, x_scale_table, x_scales, (0, 1, 2, 3))
        w1_raw = sb("w1_raw", [P, PACK, H], F32)
        nc.sync.dma_start(w1_raw[:], w1.rearrange("(p j) c -> p j c", j=PACK))
        load_words(x_word_table, x_words)
        gain = sb("gain", [P, PACK], F32)
        nc.sync.dma_start(gain[:], gn.rearrange("(p t) o -> p (t o)", t=PACK))
        k1_l = load_list("k1_l", k1)
        nc.sync.dma_start(d_scale_table[0:P:8, :].bitcast(I32), d_scales[0].bitcast(I32))
        load_words(d_word_table, d_words)
        n1_l = load_list("n1_l", n1)
        n2_l = load_list("n2_l", n2)
        w2_raw = sb("w2_raw", [P, PACK, N], F32)
        nc.sync.dma_start(w2_raw[:], w2.rearrange("(p j) c -> p j c", j=PACK))
        n5_l = load_list("n5_l", n5)
        n3_l = load_list("n3_l", n3)
        n4_l = load_list("n4_l", n4)

        twice_nonneg = sb("twice_nonneg", [P, PACK], F32)
        gain_sign = sb("gain_sign", [P, PACK], F32)
        gain_size = sb("gain_size", [P, PACK], F32)
        nc.gpsimd.tensor_scalar(twice_nonneg[:], gain[:], 0.0, 2.0, ALU.is_ge, ALU.mult)
        nc.gpsimd.tensor_scalar(gain_sign[:], twice_nonneg[:], 1.0, -1.0, ALU.mult, ALU.add)
        nc.scalar.activation(gain_size[:], gain[:], mybir.ActivationFunctionType.Abs)

        xo_scales = sb("xo_scales", [P, S], U8)
        xo_words = sb("xo_words", [P, S], U32)
        nc.vector.tensor_copy(xo_scales[:], x_scale_table[:].indirect(offs_l[:]))
        nc.vector.tensor_copy(xo_words[:], x_word_table[:].indirect(offs_l[:]))

        w1_bf = sb("w1_bf", [P, PACK, P, PACK], BF16)
        w1_dealt = w1_bf[:].rearrange("p t m j -> p m j t")
        w1_rows = w1_raw[:].rearrange("p j (m t) -> p m j t", t=PACK)
        nc.scalar.activation(w1_dealt[:, :SM], w1_rows[:, :SM], COPY)
        nc.vector.tensor_copy(w1_dealt[:, SM:], w1_rows[:, SM:])
        w1_codes = sb("w1_codes", [P, H], U32)
        w1_scales = sb("w1_scales", [P, H], U8)
        for t in ORDER:
            cols = slice(t * P, (t + 1) * P)
            nc.vector.quantize_mx(
                out=w1_codes[:, cols].bitcast(FP8X4),
                scales=w1_scales[:, cols],
                in_=w1_bf[:, t].rearrange("p m j -> p (m j)"),
            )

        def project(t):
            y_bank = psum.tile([P, S], F32, name="y_bank", tag="bank%d" % t)
            mx(y_bank[:], w1_codes, w1_scales, t, xo_words[:], xo_scales[:])
            nc.scalar.activation(y_win[t][:, :S], y_bank[:], COPY, scale=gain_size[:, t : t + 1])

        xt_scales = sb("xt_scales", [P, S], U8)
        xt_words = sb("xt_words", [P, S], U32)
        dk_scales = sb("dk_scales", [P, H], U8)
        dk_words = sb("dk_words", [P, H], U32)
        dk_scales_dealt = sb("dk_scales_dealt", [P, H], U8)
        dk_words_dealt = sb("dk_words_dealt", [P, H], U32)
        nc.vector.tensor_copy(xt_scales[:], x_scale_table[:].indirect(two_l[:]))
        nc.vector.tensor_copy(xt_words[:], x_word_table[:].indirect(two_l[:]))

        def pick_code_scales():
            nc.vector.tensor_copy(dk_scales[:], d_scale_table[:].indirect(k1_l[:]))

        def deal_code_scales():
            nc.vector.tensor_copy(
                dk_scales_dealt[:].rearrange("p (t m) -> p m t", t=PACK),
                dk_scales[:].rearrange("p (m t) -> p m t", t=PACK),
            )
            for r, place in enumerate((0, 8, 16, 24)):
                nc.sync.dma_start(d_scale_placed[r:P:32, :].bitcast(I32), dk_scales_dealt[place:P:32, :].bitcast(I32))

        def pick_code_words():
            nc.vector.tensor_copy(dk_words[:], d_word_table[:].indirect(k1_l[:]))

        def deal_code_words():
            nc.vector.tensor_copy(
                dk_words_dealt[:].rearrange("p (t m) -> p m t", t=PACK),
                dk_words[:].rearrange("p (m t) -> p m t", t=PACK),
            )

        def members(t):
            mb = ring.tile([P, W], F32, name="mb")
            for h in range(2):
                gather(h == 1 and t in VG, mb[:, h * S : (h + 1) * S], y_win[t][:], n1_l[:, h * 32 : (h + 1) * 32])
            return mb

        def difference_last(mb):
            pairs = mb[:].rearrange("p (h j e) -> p h e j", h=2, e=2)
            late_half = keep.tile([P, S // 2], F32, name="late_half", tag="w2_bf", align_bytes=64)
            held = [b_win[3][:, : S // 2], late_half[:]]
            for h in range(2):
                nc.vector.tensor_tensor(held[h], pairs[:, h, 0], pairs[:, h, 1], ALU.max)
            for h in range(2):
                cols = slice(h * (S // 2), (h + 1) * (S // 2))
                nc.vector.tensor_tensor(st_all[:, cols], y_win[0][:, cols], held[h], ALU.subtract)

        def difference(t, mb):
            pairs = mb[:].rearrange("p (j e) -> p e j", e=2)
            nc.vector.tensor_tensor(larger[t], pairs[:, 0], pairs[:, 1], ALU.max)
            nc.vector.tensor_tensor(st_all[:, t * S : (t + 1) * S], y_win[t][:, :S], larger[t], ALU.subtract)

        def partner(t):
            gather(False, st2_all[:, t * S : (t + 1) * S], st_all[:, t * S : (t + 2) * S], n2_l[:])

        late = {}
        w2_codes = sb("w2_codes", [P, N], U32)
        w2_scales = sb("w2_scales", [P, N], U8)

        def round_w2():
            w2_bf = keep.tile([P, PACK, P, PACK], BF16, name="w2_bf", tag="w2_bf", align_bytes=64)
            late["w2_bf"] = w2_bf
            dealt = w2_bf[:].rearrange("p t (q m) j -> p q m j t", q=WQ)
            raw = w2_raw[:].rearrange("p j (q m t) -> p q m j t", q=WQ, t=PACK)
            sign = gain_sign[:].unsqueeze(1).unsqueeze(3).to_broadcast([P, P // WQ, PACK, PACK])
            for q in range(WQ):
                nc.vector.tensor_tensor(dealt[:, q], raw[:, q], sign, ALU.mult)

        def quantize_w2():
            nc.vector.quantize_mx(
                out=w2_codes[:].bitcast(FP8X4), scales=w2_scales[:], in_=late["w2_bf"][:].rearrange("p t m j -> p (t m j)")
            )

        b_banks = {}

        def coded(t):
            b_bank = psum.tile([P, S], F32, name="b_bank", tag="bank%d" % (PACK + t))
            mx(b_bank[:], dk_words_dealt, d_scale_placed, t, xt_words[:], xt_scales[:])
            nc.scalar.activation(b_win[t][:, :S], b_bank[:], COPY, scale=0.5 * 0.0625)
            b_banks[t] = b_bank

        def fetch_coded(t):
            gather(t in VG5, a_win[t][:, S:], b_win[t][:], n5_l[:])

        mbs = {}
        project(3)
        mbs[3] = members(3)
        project(2)
        mbs[2] = members(2)
        difference(3, mbs[3])
        partner(3)
        project(1)
        mbs[1] = members(1)
        difference(2, mbs[2])
        partner(2)
        project(0)
        mbs[0] = members(0)
        difference(1, mbs[1])
        partner(1)
        difference_last(mbs[0])
        partner(0)
        pick_code_scales()
        pick_code_words()
        deal_code_scales()
        deal_code_words()
        round_w2()
        quantize_w2()
        coded(3)
        coded(2)
        coded(1)
        fetch_coded(3)
        fetch_coded(2)

        z_codes = sb("z_codes", [P, S], U32)
        z_scales = sb("z_scales", [P, S], U8)
        z_bf = [keep.tile([P, S // 2, PACK], BF16, name="z_bf", tag="z_bf%d" % h, align_bytes=64) for h in range(2)]
        st_view = st_all[:, : PACK * S].rearrange("p (t h c i) -> p h c t i", t=PACK, h=2, i=4)
        st2_view = st2_all[:].rearrange("p (t h c i) -> p h c t i", t=PACK, h=2, i=4)
        for h in range(2):
            z_view = z_bf[h][:].rearrange("p (c i) t -> p c t i", i=4)
            nc.vector.tensor_tensor(z_view, st_view[:, h], st2_view[:, h], ALU.max)
        for h in range(2):
            cols = slice(h * (S // 2), (h + 1) * (S // 2))
            nc.vector.quantize_mx(
                out=z_codes[:, cols].bitcast(FP8X4),
                scales=z_scales[:, cols],
                in_=z_bf[h][:].rearrange("p c t -> p (c t)"),
            )
        a_win[1] = keep.tile([P, 2 * S], F32, name="a_win1", tag="z_bf1", align_bytes=64)
        fetch_coded(1)

        out_rows = out.rearrange("(p t) n -> t p n", t=PACK)
        a_banks, seconds = {}, {}

        def second_term(t):
            a_bank = psum.tile([P, S], F32, name="a_bank", tag="bank%d" % t)
            mx(a_bank[:], w2_codes, w2_scales, t, z_codes[:], z_scales[:])
            if t in VEV:
                nc.vector.tensor_copy(a_win[t][:, :S], a_bank[:])
            else:
                nc.scalar.activation(a_win[t][:, :S], a_bank[:], COPY)
            if t == 2:
                coded(0)
                fetch_coded(0)
            at_n4 = ring.tile([P, S], F32, name="at_n4")
            step4 = ring.tile([P, S], F32, name="step4")
            second = ring.tile([P, S], F32, name="second")
            gather(t in VG4, at_n4[:], a_win[t][:], n4_l[:])
            nc.vector.tensor_tensor(step4[:], at_n4[:], a_bank[:], ALU.subtract)
            nc.gpsimd.tensor_tensor(second[:], step4[:], a_win[t][:, S:], ALU.mult)
            a_banks[t], seconds[t] = a_bank, second

        def first_term(t):
            at_n3 = ring.tile([P, S], F32, name="at_n3")
            step3 = ring.tile([P, S], F32, name="step3")
            first = ring.tile([P, S], F32, name="first")
            result = ring.tile([P, S], F32, name="result")
            closer = nc.vector if t in VR else nc.gpsimd
            pieces = LASTP if t == 0 else 1
            width = S // pieces
            spans = [slice(k * width, (k + 1) * width) for k in range(pieces)]
            for cols in spans:
                gather(t in VG3, at_n3[:, cols], a_win[t][:], n3_l[:, cols.start // 16 : cols.stop // 16])
                nc.vector.tensor_tensor(step3[:, cols], at_n3[:, cols], a_banks[t][:, cols], ALU.subtract)
            for cols in spans:
                nc.vector.scalar_tensor_tensor(
                    first[:, cols], b_banks[t][:, cols], 0.0625, step3[:, cols], ALU.mult, ALU.mult
                )
            for cols in spans:
                closer.tensor_tensor(result[:, cols], first[:, cols], seconds[t][:, cols], ALU.add)
                nc.sync.dma_start(out_rows[t][:, cols], result[:, cols])

        second_term(3)
        first_term(3)
        second_term(2)
        first_term(2)
        second_term(1)
        first_term(1)
        second_term(0)
        first_term(0)
